import numpy as np
import ml_dtypes


def mxq(x, axis, fmt="e4m3"):
    dtype, down = {"e4m3": (ml_dtypes.float8_e4m3fn, 7), "e5m2": (ml_dtypes.float8_e5m2, 14)}[fmt]
    v = np.moveaxis(np.asarray(x, np.float32).astype(ml_dtypes.bfloat16).astype(np.float64), axis, -1)
    blocks = v.reshape(v.shape[:-1] + (-1, 32))
    amax = np.abs(blocks).max(-1, keepdims=True)
    byte = np.maximum(np.where(amax > 0, np.frexp(amax)[1] - 1 + 127, 0) - down, 1)
    scale = np.exp2(byte - 127.0)
    codes = (blocks / scale).astype(np.float32).astype(dtype).astype(np.float64)
    return np.moveaxis((codes * scale).reshape(v.shape), -1, axis)


WIDE = False


def mx_kscale(k):
    if not WIDE:
        return np.ones(k)
    levels = np.array([10, -10, 5, -5, 0])
    if k % 512:
        return np.exp2(np.random.permutation(np.resize(levels, k // 32))).repeat(32)
    a = np.empty((k // 512, 16))
    for p in range(k // 512):
        a[p, :8] = np.random.permutation(np.resize(levels, 8))
        for g in range(8):
            far = levels[np.abs(levels - a[p, g]) >= 10]
            a[p, g + 8] = far[np.random.randint(len(far))]
    return np.exp2(a.ravel()).repeat(32)


BF16 = ml_dtypes.bfloat16


def bf(x):
    return np.asarray(x, np.float32).astype(BF16)


def f64(x):
    return np.asarray(x).astype(np.float64)

def planes(Y):
    n, m = Y.shape
    b = f64(bf(Y)).reshape(n // 32, 32, m)
    amax = np.abs(b).max(1)
    byte = np.clip(np.where(amax > 0, np.frexp(amax)[1] - 1 + 127 - 7, 1), 1, 254)
    codes = (b * np.exp2(127.0 - byte)[:, None, :]).reshape(n, m).astype(np.float32).astype(ml_dtypes.float8_e4m3fn).view(np.uint8)
    words = codes.reshape(n // 512, 128, 4, m).transpose(0, 1, 3, 2)
    return np.ascontiguousarray(words), np.ascontiguousarray(byte.astype(np.uint8).reshape(n // 512, 16, m))


B, H, W, F = 2, 1024, 1024, 512


def setup_inputs():
    s = mx_kscale(W)
    images = np.random.randn(B, H, W) * s
    even = np.random.randn(W, F) / np.sqrt(W) / s[:, None]
    odd = np.random.randn(W, F) / np.sqrt(W) / s[:, None]
    shift = np.random.randn(H, 1)
    freq = np.random.uniform(0.2, np.pi, (1, F))
    window = np.exp(0.8 * np.random.randn(H))
    return {"images": bf(images), "even": bf(even), "odd": bf(odd),
            "cos_tab": bf(np.cos(shift * freq)),
            "sin_tab": bf(np.sin(shift * freq)),
            "window": bf(window)}

def reference(images, even, odd, cos_tab, sin_tab, window):
    xq = mxq(f64(images).reshape(B * H, W), 1, "e4m3")
    u = (xq @ mxq(f64(even), 0, "e4m3")).reshape(B, H, F)
    v = (xq @ mxq(f64(odd), 0, "e4m3")).reshape(B, H, F)
    y = (u * f64(cos_tab) + v * f64(sin_tab)) * f64(window).reshape(H, 1)
    Y = y.transpose(1, 0, 2).reshape(H, B * F)
    words, scales = planes(Y)
    return y, words, scales

@@ -1,0 +1,293 @@
+from contextlib import ExitStack
+
+import concourse.mybir as mybir
+from concourse.masks import make_identity
+
+F32 = mybir.dt.float32
+BF16 = mybir.dt.bfloat16
+U32 = mybir.dt.uint32
+I32 = mybir.dt.int32
+U8 = mybir.dt.uint8
+FP8X4 = mybir.dt.float8_e4m3fn_x4
+MULT = mybir.AluOpType.mult
+ADD = mybir.AluOpType.add
+
+B, H, W, F = 2, 1024, 1024, 512
+FLOPS = 2 * 2 * B * H * W * F
+P = 128
+BANKS = 8
+
+SP = "we0 x0-2 we1 x2-4 wo0 wo1 x4-6 c0:0-2 win s0:0-2 x6-8 x8-10 x12-14 s0:2-4 c0:2-4 x10-12 s1 c1 y0-2 x14-16 y2-4 y4-6 o0 y6-8 o1 z0 y8-10 y10-12 va12-14 va14-16 vb12-14 vb14-16 o2 o3a o3b z1"
+PE = "T1 T0 T3 T2 U0 U1 T4 T5 V0 V1 T7 T6 V2 U2 U3 V3 U4 V4 T9 T8 V5 U5 U6 U7 V6 T11 V7 V8 U8 T10 T12 T13 U9 V9 V10 U11 U10 T15 T14 V11 Ha12 Ha13 Hb12 Hb13 Ha15 Ha14 Hb15 Hb14"
+SC = "E1 E0 Io0b Io1b E2 E3 E4 E5 E6 E8 E9 C0a C0b E11 E10 C1a E13 E12 C1b E14 E15 C2a C2b C3a C3f"
+VE = "Ie0a Ie0b We0 Ie1b Ie1a X0-2 We1 Io0a Io1a Wo0 Wo1 P0 X2-4 R0 X4-6 P1 R1 E7 R2 P2 X6-8 R3 P3 P4 R4 R5 P5 P6 X8-10 R6 A5-6 P7 R7 Y0 P8 R8 X10-12 P9 R9 R10 P11 P10 X12-14 A10-11 Y1 R11 X14-16 Qa13 Qa12 Qb12 Qa15 Qa14 Qb13 Ba14-16 Qb15 Qb14 Bb14-16 Y2 C3e Y3a Y3b"
+GP = "A0-1 A1-2 A2-3 A3-4 A4-5 A6-7 A7-8 A8-9 A9-10 A11-12 Ba12-14 Bb12-14"
+
+
+def tile_sheared_right_basis_transform_g2_kernel(tc, images, even, odd, cos_tab, sin_tab, window, out_0, out_1, out_2):
+    nc = tc.nc
+    with ExitStack() as ctx:
+        sb = ctx.enter_context(tc.tile_pool(name="sb", bufs=1))
+        ps = ctx.enter_context(tc.psum_pool(name="ps", bufs=1))
+
+        def tiles(name, count, shape, dtype):
+            return [sb.tile(shape, dtype, name="%s%d" % (name, i), align_bytes=64) for i in range(count)]
+
+        ident = sb.tile([P, P], F32, name="ident")
+        win = sb.tile([P, 2, 4], BF16, name="win")
+        x_raw = tiles("x_raw", 4, [P, 4, W], BF16)
+        x_grp = tiles("x_grp", 2, [P, 4, W], BF16)
+        x_codes = tiles("x_codes", 4, [P, 4 * 256], U32)
+        x_scales = tiles("x_scales", 4, [P, 4 * 256], U8)
+        w_raw = tiles("w_raw", 4, [P, 4, F], BF16)
+        w_grp = tiles("w_grp", 4, [P, F, 4], BF16)
+        w_codes = tiles("w_codes", 4, [P, F], U32)
+        w_scales = tiles("w_scales", 4, [P, F], U8)
+        tabs = tiles("tabs", 2, [P, 2, 4, F], BF16)
+        prod = tiles("prod", 4, [P, 2, 4, F], F32)
+        cos_sb = [t[:, 0] for t in tabs]
+        sin_sb = [t[:, 1] for t in tabs]
+        y = [t[:, 0] for t in prod]
+        vs = [t[:, 1] for t in prod]
+        y_grp = tiles("y_grp", 2, [P, F, 4], BF16)
+        y_codes = tiles("y_codes", 4, [P, F], U32)
+        y_scales = tiles("y_scales", 2, [P, B * F], U8)
+        banks = [ps.tile([P, 512], F32, name="bank%d" % i) for i in range(BANKS)]
+
+        bank_of = {}
+        for i, step in enumerate(PE.split()):
+            bank_of[step] = i % BANKS
+        pe_steps = PE.split()
+        reader = {"T": "E", "U": "P", "V": "R", "H": "Q"}
+
+        def span(text):
+            lo, hi = text.split("-")
+            return int(lo), int(hi)
+
+        def half(letter):
+            return {"a": (0, 256), "b": (256, 512), "c": (0, 128), "d": (128, 256), "e": (256, 384), "f": (384, 512)}[letter]
+
+        def widx(text):
+            return {"e": 0, "o": 2}[text[0]] + int(text[1])
+
+        def rows(ap):
+            return ap.rearrange("(p t) c -> p t c", t=4)
+
+        def emit(eng, step):
+            kind, arg = step[0], step[1:]
+            if step == "win":
+                eng.dma_start(out=win[:], in_=window.rearrange("(g p t) -> p g t", g=2, t=4))
+            elif kind == "x":
+                lo, hi = span(arg)
+                grp = lo // 4
+                g, b = divmod(grp, 2)
+                eng.dma_start(out=x_raw[grp][:, lo % 4 : lo % 4 + hi - lo, :], in_=rows(images[b, 512 * g : 512 * g + 512, :])[:, lo % 4 : lo % 4 + hi - lo, :])
+            elif kind == "w":
+                kg = int(arg[1])
+                src = even if arg[0] == "e" else odd
+                eng.dma_start(out=w_raw[widx(arg)][:], in_=rows(src[512 * kg : 512 * kg + 512, :]))
+            elif kind in "cs":
+                g = int(arg[0])
+                lo, hi = span(arg[2:]) if len(arg) > 1 else (0, 4)
+                src, dst = (cos_tab, cos_sb) if kind == "c" else (sin_tab, sin_sb)
+                eng.dma_start(out=dst[g][:, lo:hi, :], in_=rows(src[512 * g : 512 * g + 512, :])[:, lo:hi, :])
+            elif kind == "y":
+                lo, hi = span(arg)
+                grp = lo // 4
+                g, b = divmod(grp, 2)
+                eng.dma_start(out=rows(out_0[b, 512 * g : 512 * g + 512, :])[:, lo % 4 : lo % 4 + hi - lo, :], in_=y[grp][:, lo % 4 : lo % 4 + hi - lo, :])
+            elif kind == "v":
+                c0, c1 = half(arg[0])
+                lo, hi = span(arg[1:])
+                grp = lo // 4
+                g, b = divmod(grp, 2)
+                eng.dma_start(out=rows(out_0[b, 512 * g : 512 * g + 512, :])[:, lo % 4 : lo % 4 + hi - lo, c0:c1], in_=y[grp][:, lo % 4 : lo % 4 + hi - lo, c0:c1])
+            elif kind == "H":
+                c0, c1 = half(arg[0])
+                s = int(arg[1:])
+                bank = banks[bank_of[step]]
+                for side in range(2):
+                    for kg in range(2):
+                        cols = slice(256 * (s % 4) + 128 * kg, 256 * (s % 4) + 128 * kg + 128)
+                        wi = 2 * side + kg
+                        eng.matmul_mx(out=bank[:, side * (c1 - c0) : (side + 1) * (c1 - c0)], lhsT=x_codes[s // 4][:, cols].bitcast(FP8X4), lhsT_scale=x_scales[s // 4][:, cols],
+                                      rhs=w_codes[wi][:, c0:c1].bitcast(FP8X4), rhs_scale=w_scales[wi][:, c0:c1], start=(kg == 0), stop=(kg == 1))
+            elif kind == "Q":
+                c0, c1 = half(arg[0])
+                s = int(arg[1:])
+                g = s // 8
+                bank = banks[bank_of["H" + arg]]
+                eng.scalar_tensor_tensor(out=prod[s // 4][:, :, s % 4, c0:c1], in0=bank[:, : 2 * (c1 - c0)].rearrange("p (a f) -> p a f", a=2),
+                                         scalar=win[:, g, s % 4 : s % 4 + 1], in1=tabs[g][:, :, s % 4, c0:c1], op0=MULT, op1=MULT)
+            elif kind == "B":
+                c0, c1 = half(arg[0])
+                lo, hi = span(arg[1:])
+                grp = lo // 4
+                ts = slice(lo % 4, lo % 4 + hi - lo)
+                eng.tensor_tensor(out=y[grp][:, ts, c0:c1], in0=y[grp][:, ts, c0:c1], in1=vs[grp][:, ts, c0:c1], op=ADD)
+            elif kind == "o":
+                grp = int(arg[0])
+                g, b = divmod(grp, 2)
+                lo, hi = half(arg[1]) if len(arg) > 1 else (0, 512)
+                words = out_1[g].rearrange("p m t -> p (m t)").bitcast(I32)
+                eng.dma_start(out=words[:, F * b + lo : F * b + hi], in_=y_codes[grp][:, lo:hi].bitcast(I32))
+            elif kind == "z":
+                g = int(arg[0])
+                quads = [int(q) for q in arg[1:]] if len(arg) > 1 else range(4)
+                for q in quads:
+                    eng.dma_start(out=out_2[g, 4 * q : 4 * q + 4, :].bitcast(I32), in_=y_scales[g][32 * q : 32 * q + 4, :].bitcast(I32))
+            elif kind == "T":
+                s = int(arg)
+                words = x_raw[s // 4][:, s % 4, :].bitcast(F32)
+                bank = banks[bank_of[step]]
+                for kg in range(2):
+                    for u in range(2):
+                        j = 2 * kg + u
+                        eng.transpose(bank[:, 128 * j : 128 * j + 128], words[:, 256 * kg + u : 256 * kg + 256 : 2], ident[:])
+            elif kind in "UV":
+                s = int(arg)
+                bank = banks[bank_of[step]]
+                for kg in range(2):
+                    cols = slice(256 * (s % 4) + 128 * kg, 256 * (s % 4) + 128 * kg + 128)
+                    wi = (0 if kind == "U" else 2) + kg
+                    eng.matmul_mx(out=bank[:], lhsT=x_codes[s // 4][:, cols].bitcast(FP8X4), lhsT_scale=x_scales[s // 4][:, cols],
+                                  rhs=w_codes[wi][:].bitcast(FP8X4), rhs_scale=w_scales[wi][:], start=(kg == 0), stop=(kg == 1))
+            elif kind == "E":
+                s = int(arg)
+                bank = banks[bank_of["T" + arg]]
+                dst = x_grp[(s // 4) % 2][:, s % 4, :].bitcast(F32).rearrange("p (kg r u) -> p kg r u", kg=2, u=2)
+                src = bank[:].rearrange("p (kg u r) -> p kg r u", kg=2, u=2)
+                if eng is nc.scalar:
+                    eng.copy(out=dst, in_=src)
+                else:
+                    eng.tensor_copy(out=dst, in_=src)
+            elif kind == "I":
+                wi = widx(arg)
+                lo, hi = half(arg[2])
+                dst = w_grp[wi][:, lo:hi, :].rearrange("p (c i) t -> p c t i", i=4)
+                src = w_raw[wi][:, :, lo:hi].rearrange("p t (c i) -> p c t i", i=4)
+                if eng is nc.scalar:
+                    eng.copy(out=dst, in_=src)
+                else:
+                    eng.tensor_copy(out=dst, in_=src)
+            elif kind == "W":
+                wi = widx(arg)
+                eng.quantize_mx(out=w_codes[wi][:].bitcast(FP8X4), scales=w_scales[wi][:], in_=w_grp[wi][:].rearrange("p f t -> p (f t)"))
+            elif kind == "X":
+                lo, hi = span(arg)
+                grp = lo // 4
+                cols = slice(256 * (lo % 4), 256 * (lo % 4 + hi - lo))
+                eng.quantize_mx(out=x_codes[grp][:, cols].bitcast(FP8X4), scales=x_scales[grp][:, cols],
+                                in_=x_grp[grp % 2][:, lo % 4 : lo % 4 + hi - lo, :].rearrange("p t w -> p (t w)"))
+            elif kind in "PR":
+                s = int(arg)
+                g = s // 8
+                bank = banks[bank_of[("U" if kind == "P" else "V") + arg]]
+                dst = y[s // 4] if kind == "P" else vs[s // 4]
+                tab = cos_sb if kind == "P" else sin_sb
+                eng.scalar_tensor_tensor(out=dst[:, s % 4, :], in0=bank[:], scalar=win[:, g, s % 4 : s % 4 + 1], in1=tab[g][:, s % 4, :], op0=MULT, op1=MULT)
+            elif kind == "A":
+                lo, hi = span(arg)
+                grp = lo // 4
+                ts = slice(lo % 4, lo % 4 + hi - lo)
+                eng.tensor_tensor(out=y[grp][:, ts, :], in0=y[grp][:, ts, :], in1=vs[grp][:, ts, :], op=ADD)
+            elif kind == "C":
+                grp = int(arg[0])
+                lo, hi = half(arg[1])
+                dst = y_grp[grp % 2][:, lo:hi, :].rearrange("p (c i) t -> p c t i", i=2)
+                src = y[grp][:, :, lo:hi].rearrange("p t (c i) -> p c t i", i=2)
+                if eng is nc.scalar:
+                    eng.copy(out=dst, in_=src)
+                else:
+                    eng.tensor_copy(out=dst, in_=src)
+            elif kind == "Y":
+                grp = int(arg[0])
+                g, b = divmod(grp, 2)
+                lo, hi = half(arg[1]) if len(arg) > 1 else (0, 512)
+                eng.quantize_mx(out=y_codes[grp][:, lo:hi].bitcast(FP8X4), scales=y_scales[g][:, F * b + lo : F * b + hi],
+                                in_=y_grp[grp % 2][:, lo:hi, :].rearrange("p f t -> p (f t)"))
+
+        queues = [(nc.sync, SP.split()), (nc.tensor, pe_steps), (nc.scalar, SC.split()), (nc.vector, VE.split()), (nc.gpsimd, GP.split())]
+        every = [step for eng, steps in queues for step in steps]
+
+        def covering(kind, s):
+            return [t for t in every if t[0] == kind and ":" not in t and "-" in t and span(t[1:])[0] <= s < span(t[1:])[1]]
+
+        def cols_meet(a, b):
+            la, ha = half(a) if a else (0, 512)
+            lb, hb = half(b) if b else (0, 512)
+            return la < hb and lb < ha
+
+        def cover_b(s, letter):
+            return [t for t in every if t[0] == "B" and cols_meet(t[1], letter) and span(t[2:])[0] <= s < span(t[2:])[1]]
+
+        def needs(step):
+            kind, arg = step[0], step[1:]
+            if kind == "Q":
+                return ["H" + arg, "win"] + [t for t in every if t[0] in "cs" and t[1] == "1"]
+            if kind == "B":
+                lo, hi = span(arg[1:])
+                return [t for t in every if t[0] == "Q" and cols_meet(t[1], arg[0]) and lo <= int(t[2:]) < hi]
+            if kind == "v":
+                lo, hi = span(arg[1:])
+                return [t for s in range(lo, hi) for t in cover_b(s, arg[0])]
+            if step == "win" or kind in "xwcs":
+                return []
+            if kind in "TUVH":
+                i = pe_steps.index(step)
+                out = []
+                if i >= BANKS:
+                    old = pe_steps[i - BANKS]
+                    out.append(reader[old[0]] + old[1:])
+                if kind == "H":
+                    return out + covering("X", int(arg[1:])) + ["We0", "We1", "Wo0", "Wo1"]
+                s = int(arg)
+                if kind == "T":
+                    return out + covering("x", s)
+                return out + covering("X", s) + ["W" + ("e" if kind == "U" else "o") + str(kg) for kg in range(2)]
+            if kind == "E":
+                s = int(arg)
+                return ["T" + arg] + (covering("X", s - 8) if s >= 8 else [])
+            if kind == "I":
+                return ["w" + arg[:2]]
+            if kind == "W":
+                return [t for t in every if t[0] == "I" and t[1:3] == arg]
+            if kind == "X":
+                lo, hi = span(arg)
+                return ["E%d" % s for s in range(lo, hi)]
+            if kind in "PR":
+                s = int(arg)
+                tab = "c" if kind == "P" else "s"
+                out = [("U" if kind == "P" else "V") + arg, "win"] + [t for t in every if t[0] == tab and t[1] == str(s // 8)]
+                return out
+            if kind == "A":
+                lo, hi = span(arg)
+                return ["P%d" % s for s in range(lo, hi)] + ["R%d" % s for s in range(lo, hi)]
+            if kind == "y":
+                lo, hi = span(arg)
+                return [t for s in range(lo, hi) for t in covering("A", s) + cover_b(s, "")]
+            if kind == "C":
+                grp = int(arg[0])
+                old = [t for t in every if t[0] == "Y" and int(t[1]) == grp - 2]
+                return old + [t for s in range(4 * grp, 4 * grp + 4) for t in covering("A", s) + cover_b(s, arg[1])]
+            if kind == "Y":
+                return [t for t in every if t[0] == "C" and t[1] == arg[0] and cols_meet(t[2:], arg[1:])]
+            if kind == "o":
+                return [t for t in every if t[0] == "Y" and t[1] == arg[0] and cols_meet(t[2:], arg[1:])]
+            if kind == "z":
+                return [t for t in every if t[0] == "Y" and int(t[1]) // 2 == int(arg[0])]
+
+        make_identity(nc, ident[:])
+        with tc.manual_schedule():
+            if True:
+                done = set()
+                at = [0] * len(queues)
+                while len(done) < len(every):
+                    moved = False
+                    for qi, (eng, steps) in enumerate(queues):
+                        while at[qi] < len(steps) and all(t in done for t in needs(steps[at[qi]])):
+                            emit(eng, steps[at[qi]])
+                            done.add(steps[at[qi]])
+                            at[qi] += 1
+                            moved = True
+                    assert moved

@@ -17,11 +17,11 @@ FLOPS = 2 * 2 * B * H * W * F
 P = 128
 BANKS = 8
 
-SP = "we0 x0-2 we1 x2-4 wo0 wo1 x4-6 c0:0-2 win s0:0-2 x6-8 x8-10 x12-14 s0:2-4 c0:2-4 x10-12 s1 c1 y0-2 x14-16 y2-4 y4-6 o0 y6-8 o1 z0 y8-10 y10-12 va12-14 va14-16 vb12-14 vb14-16 o2 o3a o3b z1"
-PE = "T1 T0 T3 T2 U0 U1 T4 T5 V0 V1 T7 T6 V2 U2 U3 V3 U4 V4 T9 T8 V5 U5 U6 U7 V6 T11 V7 V8 U8 T10 T12 T13 U9 V9 V10 U11 U10 T15 T14 V11 Ha12 Ha13 Hb12 Hb13 Ha15 Ha14 Hb15 Hb14"
-SC = "E1 E0 Io0b Io1b E2 E3 E4 E5 E6 E8 E9 C0a C0b E11 E10 C1a E13 E12 C1b E14 E15 C2a C2b C3a C3f"
-VE = "Ie0a Ie0b We0 Ie1b Ie1a X0-2 We1 Io0a Io1a Wo0 Wo1 P0 X2-4 R0 X4-6 P1 R1 E7 R2 P2 X6-8 R3 P3 P4 R4 R5 P5 P6 X8-10 R6 A5-6 P7 R7 Y0 P8 R8 X10-12 P9 R9 R10 P11 P10 X12-14 A10-11 Y1 R11 X14-16 Qa13 Qa12 Qb12 Qa15 Qa14 Qb13 Ba14-16 Qb15 Qb14 Bb14-16 Y2 C3e Y3a Y3b"
-GP = "A0-1 A1-2 A2-3 A3-4 A4-5 A6-7 A7-8 A8-9 A9-10 A11-12 Ba12-14 Bb12-14"
+SP = "we0 x0-2 we1 x2-4 wo0 wo1 x4-6 x6-8 win c0:0-2 s0:0-2 x8-10 c0:2-4 s0:2-4 x10-12 x12-14 c1 s1 x14-16 y0-2 y2-4 y4-6 o0 y6-8 y8-10 y10-12 va12-14 va14-16 o1 z0 vb12-14 vb14-16 o2 o3a o3b z101"
+PE = "T0 T1 T2 T3 U0 U1 T4 T5 T6 T7 V0 V1 U2 V2 T8 T9 U3 V3 U4 V4 T10 T11 U5 V5 U6 V6 U7 V7 U8 V8 T12 T13 U9 V9 U10 V10 T14 T15 U11 V11 Ha12 Ha13 Ha14 Ha15 Hb12 Hb13 Hb14 Hb15"
+SC = "Ie0b E0 Ie1b E2 E3 Io1b E4 E5 E6 E7 E8 E9 E10 E11 C0a C0b E12 E13 E14 E15 C1a C1b C2a C2b C3a C3e z123"
+VE = "Ie0a We0 Ie1a E1 X0-2 We1 Io0a Io0b Io1a Wo0 Wo1 X2-4 P0 P1 X4-6 R0 R1 X6-8 R2 P2 P3 R3 X8-10 R4 P4 P5 R5 X10-12 R6 P6 P7 R7 Y0 R8 P8 P9 R9 X12-14 R10 P10 P11 R11 X14-16 Qa12 Qa13 Qa14 Qa15 Qb12 Qb13 Qb14 Qb15 Y1 Bb12-14 Bb14-16 Y2 C3f Y3a Y3b"
+GP = "A0-2 Ba2-4 Bb2-4 A4-6 A6-8 A8-10 A10-12 Ba12-14 Ba14-16"
 
 
 def tile_sheared_right_basis_transform_g2_kernel(tc, images, even, odd, cos_tab, sin_tab, window, out_0, out_1, out_2):
@@ -49,16 +49,20 @@ def tile_sheared_right_basis_transform_g2_kernel(tc, images, even, odd, cos_tab,
         sin_sb = [t[:, 1] for t in tabs]
         y = [t[:, 0] for t in prod]
         vs = [t[:, 1] for t in prod]
-        y_grp = tiles("y_grp", 2, [P, F, 4], BF16)
+        y_grp = tiles("y_grp", 4, [P, F, 4], BF16)
         y_codes = tiles("y_codes", 4, [P, F], U32)
         y_scales = tiles("y_scales", 2, [P, B * F], U8)
         banks = [ps.tile([P, 512], F32, name="bank%d" % i) for i in range(BANKS)]
 
         bank_of = {}
-        for i, step in enumerate(PE.split()):
-            bank_of[step] = i % BANKS
         pe_steps = PE.split()
-        reader = {"T": "E", "U": "P", "V": "R", "H": "Q"}
+        takers = [t for t in pe_steps if t[0] != "K"]
+        for i, step in enumerate(takers):
+            bank_of[step] = i % BANKS
+            if step[0] == "G":
+                bank_of["K" + step[1:]] = i % BANKS
+                bank_of["H" + step[1:]] = i % BANKS
+        reader = {"T": "E", "U": "P", "V": "R", "H": "Q", "G": "Q"}
 
         def span(text):
             lo, hi = text.split("-")
@@ -102,11 +106,11 @@ def tile_sheared_right_basis_transform_g2_kernel(tc, images, even, odd, cos_tab,
                 grp = lo // 4
                 g, b = divmod(grp, 2)
                 eng.dma_start(out=rows(out_0[b, 512 * g : 512 * g + 512, :])[:, lo % 4 : lo % 4 + hi - lo, c0:c1], in_=y[grp][:, lo % 4 : lo % 4 + hi - lo, c0:c1])
-            elif kind == "H":
+            elif kind in "HGK":
                 c0, c1 = half(arg[0])
                 s = int(arg[1:])
                 bank = banks[bank_of[step]]
-                for side in range(2):
+                for side in {"H": (0, 1), "G": (0,), "K": (1,)}[kind]:
                     for kg in range(2):
                         cols = slice(256 * (s % 4) + 128 * kg, 256 * (s % 4) + 128 * kg + 128)
                         wi = 2 * side + kg
@@ -172,7 +176,8 @@ def tile_sheared_right_basis_transform_g2_kernel(tc, images, even, odd, cos_tab,
                     eng.tensor_copy(out=dst, in_=src)
             elif kind == "W":
                 wi = widx(arg)
-                eng.quantize_mx(out=w_codes[wi][:].bitcast(FP8X4), scales=w_scales[wi][:], in_=w_grp[wi][:].rearrange("p f t -> p (f t)"))
+                lo, hi = half(arg[2]) if len(arg) > 2 else (0, 512)
+                eng.quantize_mx(out=w_codes[wi][:, lo:hi].bitcast(FP8X4), scales=w_scales[wi][:, lo:hi], in_=w_grp[wi][:, lo:hi, :].rearrange("p f t -> p (f t)"))
             elif kind == "X":
                 lo, hi = span(arg)
                 grp = lo // 4
@@ -194,7 +199,7 @@ def tile_sheared_right_basis_transform_g2_kernel(tc, images, even, odd, cos_tab,
             elif kind == "C":
                 grp = int(arg[0])
                 lo, hi = half(arg[1])
-                dst = y_grp[grp % 2][:, lo:hi, :].rearrange("p (c i) t -> p c t i", i=2)
+                dst = y_grp[grp][:, lo:hi, :].rearrange("p (c i) t -> p c t i", i=2)
                 src = y[grp][:, :, lo:hi].rearrange("p t (c i) -> p c t i", i=2)
                 if eng is nc.scalar:
                     eng.copy(out=dst, in_=src)
@@ -205,7 +210,7 @@ def tile_sheared_right_basis_transform_g2_kernel(tc, images, even, odd, cos_tab,
                 g, b = divmod(grp, 2)
                 lo, hi = half(arg[1]) if len(arg) > 1 else (0, 512)
                 eng.quantize_mx(out=y_codes[grp][:, lo:hi].bitcast(FP8X4), scales=y_scales[g][:, F * b + lo : F * b + hi],
-                                in_=y_grp[grp % 2][:, lo:hi, :].rearrange("p f t -> p (f t)"))
+                                in_=y_grp[grp][:, lo:hi, :].rearrange("p f t -> p (f t)"))
 
         queues = [(nc.sync, SP.split()), (nc.tensor, pe_steps), (nc.scalar, SC.split()), (nc.vector, VE.split()), (nc.gpsimd, GP.split())]
         every = [step for eng, steps in queues for step in steps]
@@ -224,34 +229,36 @@ def tile_sheared_right_basis_transform_g2_kernel(tc, images, even, odd, cos_tab,
         def needs(step):
             kind, arg = step[0], step[1:]
             if kind == "Q":
-                return ["H" + arg, "win"] + [t for t in every if t[0] in "cs" and t[1] == "1"]
+                return ["H" + arg if "H" + arg in every else "K" + arg, "win"] + [t for t in every if t[0] in "cs" and t[1] == str(int(arg[1:]) // 8)]
             if kind == "B":
                 lo, hi = span(arg[1:])
-                return [t for t in every if t[0] == "Q" and cols_meet(t[1], arg[0]) and lo <= int(t[2:]) < hi]
+                return [t for t in every if t[0] == "Q" and cols_meet(t[1], arg[0]) and lo <= int(t[2:]) < hi] + [t for t in every if t[0] in "PR" and lo <= int(t[1:]) < hi]
             if kind == "v":
                 lo, hi = span(arg[1:])
                 return [t for s in range(lo, hi) for t in cover_b(s, arg[0])]
             if step == "win" or kind in "xwcs":
                 return []
-            if kind in "TUVH":
-                i = pe_steps.index(step)
+            if kind == "K":
+                return ["G" + arg] + [t for t in every if t[:2] == "Wo" and cols_meet(t[3:], arg[0])]
+            if kind in "TUVHG":
+                i = takers.index(step)
                 out = []
                 if i >= BANKS:
-                    old = pe_steps[i - BANKS]
+                    old = takers[i - BANKS]
                     out.append(reader[old[0]] + old[1:])
-                if kind == "H":
-                    return out + covering("X", int(arg[1:])) + ["We0", "We1", "Wo0", "Wo1"]
+                if kind in "HG":
+                    return out + covering("X", int(arg[1:])) + [t for t in every if t[0] == "W" and cols_meet(t[3:], arg[0]) and (kind == "H" or t[1] == "e")]
                 s = int(arg)
                 if kind == "T":
                     return out + covering("x", s)
-                return out + covering("X", s) + ["W" + ("e" if kind == "U" else "o") + str(kg) for kg in range(2)]
+                return out + covering("X", s) + [t for t in every if t[:2] == ("We" if kind == "U" else "Wo")]
             if kind == "E":
                 s = int(arg)
                 return ["T" + arg] + (covering("X", s - 8) if s >= 8 else [])
             if kind == "I":
                 return ["w" + arg[:2]]
             if kind == "W":
-                return [t for t in every if t[0] == "I" and t[1:3] == arg]
+                return [t for t in every if t[0] == "I" and t[1:3] == arg[:2] and cols_meet(t[3:], arg[2:])]
             if kind == "X":
                 lo, hi = span(arg)
                 return ["E%d" % s for s in range(lo, hi)]
@@ -268,8 +275,7 @@ def tile_sheared_right_basis_transform_g2_kernel(tc, images, even, odd, cos_tab,
                 return [t for s in range(lo, hi) for t in covering("A", s) + cover_b(s, "")]
             if kind == "C":
                 grp = int(arg[0])
-                old = [t for t in every if t[0] == "Y" and int(t[1]) == grp - 2]
-                return old + [t for s in range(4 * grp, 4 * grp + 4) for t in covering("A", s) + cover_b(s, arg[1])]
+                return [t for s in range(4 * grp, 4 * grp + 4) for t in covering("A", s) + cover_b(s, arg[1])]
             if kind == "Y":
                 return [t for t in every if t[0] == "C" and t[1] == arg[0] and cols_meet(t[2:], arg[1:])]
             if kind == "o":

@@ -17,11 +17,7 @@ FLOPS = 2 * 2 * B * H * W * F
 P = 128
 BANKS = 8
 
-SP = "we0 x0-2 we1 x2-4 wo0 wo1 x4-6 x6-8 win c0:0-2 s0:0-2 x8-10 c0:2-4 s0:2-4 x10-12 x12-14 c1 s1 x14-16 y0-2 y2-4 y4-6 o0 y6-8 y8-10 y10-12 va12-14 va14-16 o1 z0 vb12-14 vb14-16 o2 o3a o3b z101"
-PE = "T0 T1 T2 T3 U0 U1 T4 T5 T6 T7 V0 V1 U2 V2 T8 T9 U3 V3 U4 V4 T10 T11 U5 V5 U6 V6 U7 V7 U8 V8 T12 T13 U9 V9 U10 V10 T14 T15 U11 V11 Ha12 Ha13 Ha14 Ha15 Hb12 Hb13 Hb14 Hb15"
-SC = "Ie0b E0 Ie1b E2 E3 Io1b E4 E5 E6 E7 E8 E9 E10 E11 C0a C0b E12 E13 E14 E15 C1a C1b C2a C2b C3a C3e z123"
-VE = "Ie0a We0 Ie1a E1 X0-2 We1 Io0a Io0b Io1a Wo0 Wo1 X2-4 P0 P1 X4-6 R0 R1 X6-8 R2 P2 P3 R3 X8-10 R4 P4 P5 R5 X10-12 R6 P6 P7 R7 Y0 R8 P8 P9 R9 X12-14 R10 P10 P11 R11 X14-16 Qa12 Qa13 Qa14 Qa15 Qb12 Qb13 Qb14 Qb15 Y1 Bb12-14 Bb14-16 Y2 C3f Y3a Y3b"
-GP = "A0-2 Ba2-4 Bb2-4 A4-6 A6-8 A8-10 A10-12 Ba12-14 Ba14-16"
+ORDER = "SP:we0 SP:x0-2 SP:we1 SP:x2-4 SP:wo0 SP:wo1 SP:x4-6 SP:x6-8 SC:Ie0b VE:Ie0a SP:win PE:T0 SP:c0:0-2 VE:We0 PE:T1 SC:E0 VE:Ie1a SP:s0:0-2 SC:Ie1b VE:E1 PE:T2 SP:x8-10 VE:X0-2 PE:T3 SC:E2 VE:We1 SP:c0:2-4 VE:Io0a PE:U0 SC:E3 SP:s0:2-4 SC:Io1b VE:Io0b PE:U1 VE:Io1a SP:x10-12 PE:T4 VE:Wo0 PE:T5 SC:E4 VE:Wo1 SP:x12-14 PE:T6 SP:c1 SC:E5 PE:T7 VE:X2-4 SP:s1 SC:E6 VE:P0 PE:V0 SP:x14-16 PE:V1 SC:E7 VE:P1 PE:U2 VE:X4-6 PE:V2 VE:R0 PE:T8 VE:R1 PE:T9 VE:X6-8 SC:E8 PE:U3 VE:R2 GP:A0-2 SC:E9 PE:V3 VE:P2 PE:U4 VE:P3 PE:V4 VE:R3 PE:T10 VE:X8-10 SP:y0-2 PE:T11 SC:E10 VE:R4 GP:A2-4 PE:U5 SC:E11 VE:P4 PE:V5 VE:P5 PE:U6 VE:R5 PE:V6 VE:X10-12 PE:U7 SC:C0a SP:y2-4 VE:R6 GP:A4-6 PE:V7 PE:U8 VE:P6 SC:C0b PE:V8 VE:P7 PE:T12 VE:R7 PE:T13 VE:N0:0-2 SP:y4-6 SC:E12 VE:R8 GP:A6-8 PE:U9 SP:n0:0-2 SC:E13 VE:P8 PE:V9 VE:P9 PE:U10 VE:R9 PE:V10 VE:X12-14 PE:T14 SP:y6-8 PE:T15 VE:R10 GP:A8-10 SC:E14 PE:U11 VE:P10 SC:E15 PE:V11 SC:C1a VE:P11 PE:Ha12 VE:R11 PE:Ha13 SP:y8-10 VE:X14-16 SC:C1b VE:Qa12 GP:A10-12 PE:Ha14 VE:Qa13 PE:Ha15 VE:Qa14 PE:Hb12 VE:Qa15 PE:Hb13 GP:Ba12-14 VE:Qb12 PE:Hb14 SC:C2a SP:y10-12 PE:Hb15 VE:Qb13 GP:Ba14-16 VE:Qb14 SP:va12-14 SC:C2b VE:Qb15 VE:N0:2-6 SP:va14-16 SC:C3a VE:N0:6-8 VE:Bb12-14 SP:n0:2-8 VE:Bb14-16 SP:vb12-14 VE:N1:0-4 SC:C3e SP:vb14-16 VE:C3f SP:n1:0-4 VE:N1:4-6 VE:N1:6-8 SP:n1:4-6 SC:q23 SP:n1:6-8 SP:q01"
 
 
 def tile_sheared_right_basis_transform_g2_kernel(tc, images, even, odd, cos_tab, sin_tab, window, out_0, out_1, out_2):
@@ -44,25 +40,29 @@ def tile_sheared_right_basis_transform_g2_kernel(tc, images, even, odd, cos_tab,
         w_codes = tiles("w_codes", 4, [P, F], U32)
         w_scales = tiles("w_scales", 4, [P, F], U8)
         tabs = tiles("tabs", 2, [P, 2, 4, F], BF16)
-        prod = tiles("prod", 4, [P, 2, 4, F], F32)
+        prod = tiles("prod", 3, [P, 2, 4, F], F32)
+        last = tiles("last", 2, [P, 4, 2, F // 2], F32)
+
+        def last_y(ts, c0, c1, side=0):
+            return last[c0 // 256][:, ts, side, c0 % 256 : c0 % 256 + c1 - c0]
+
         cos_sb = [t[:, 0] for t in tabs]
         sin_sb = [t[:, 1] for t in tabs]
         y = [t[:, 0] for t in prod]
         vs = [t[:, 1] for t in prod]
-        y_grp = tiles("y_grp", 4, [P, F, 4], BF16)
-        y_codes = tiles("y_codes", 4, [P, F], U32)
-        y_scales = tiles("y_scales", 2, [P, B * F], U8)
+        y_grp = tiles("y_grp", 2, [P, B * F, 4], BF16)
+        y_codes = tiles("y_codes", 2, [P, B * F], U32)
+        y_scales = sb.tile([P, B * F], U8, name="y_scales", align_bytes=64)
         banks = [ps.tile([P, 512], F32, name="bank%d" % i) for i in range(BANKS)]
 
         bank_of = {}
-        pe_steps = PE.split()
+        pe_steps = [t[3:] for t in ORDER.split() if t[:2] == "PE"]
         takers = [t for t in pe_steps if t[0] != "K"]
         for i, step in enumerate(takers):
             bank_of[step] = i % BANKS
             if step[0] == "G":
                 bank_of["K" + step[1:]] = i % BANKS
                 bank_of["H" + step[1:]] = i % BANKS
-        reader = {"T": "E", "U": "P", "V": "R", "H": "Q", "G": "Q"}
 
         def span(text):
             lo, hi = text.split("-")
@@ -105,7 +105,7 @@ def tile_sheared_right_basis_transform_g2_kernel(tc, images, even, odd, cos_tab,
                 lo, hi = span(arg[1:])
                 grp = lo // 4
                 g, b = divmod(grp, 2)
-                eng.dma_start(out=rows(out_0[b, 512 * g : 512 * g + 512, :])[:, lo % 4 : lo % 4 + hi - lo, c0:c1], in_=y[grp][:, lo % 4 : lo % 4 + hi - lo, c0:c1])
+                eng.dma_start(out=rows(out_0[b, 512 * g : 512 * g + 512, :])[:, lo % 4 : lo % 4 + hi - lo, c0:c1], in_=last_y(slice(lo % 4, lo % 4 + hi - lo), c0, c1))
             elif kind in "HGK":
                 c0, c1 = half(arg[0])
                 s = int(arg[1:])
@@ -121,25 +121,22 @@ def tile_sheared_right_basis_transform_g2_kernel(tc, images, even, odd, cos_tab,
                 s = int(arg[1:])
                 g = s // 8
                 bank = banks[bank_of["H" + arg]]
-                eng.scalar_tensor_tensor(out=prod[s // 4][:, :, s % 4, c0:c1], in0=bank[:, : 2 * (c1 - c0)].rearrange("p (a f) -> p a f", a=2),
+                eng.scalar_tensor_tensor(out=last[c0 // 256][:, s % 4, :, c0 % 256 : c0 % 256 + c1 - c0], in0=bank[:, : 2 * (c1 - c0)].rearrange("p (a f) -> p a f", a=2),
                                          scalar=win[:, g, s % 4 : s % 4 + 1], in1=tabs[g][:, :, s % 4, c0:c1], op0=MULT, op1=MULT)
             elif kind == "B":
                 c0, c1 = half(arg[0])
                 lo, hi = span(arg[1:])
                 grp = lo // 4
                 ts = slice(lo % 4, lo % 4 + hi - lo)
-                eng.tensor_tensor(out=y[grp][:, ts, c0:c1], in0=y[grp][:, ts, c0:c1], in1=vs[grp][:, ts, c0:c1], op=ADD)
-            elif kind == "o":
-                grp = int(arg[0])
-                g, b = divmod(grp, 2)
-                lo, hi = half(arg[1]) if len(arg) > 1 else (0, 512)
-                words = out_1[g].rearrange("p m t -> p (m t)").bitcast(I32)
-                eng.dma_start(out=words[:, F * b + lo : F * b + hi], in_=y_codes[grp][:, lo:hi].bitcast(I32))
-            elif kind == "z":
+                eng.tensor_tensor(out=last_y(ts, c0, c1), in0=last_y(ts, c0, c1), in1=last_y(ts, c0, c1, 1), op=ADD)
+            elif kind == "n":
                 g = int(arg[0])
-                quads = [int(q) for q in arg[1:]] if len(arg) > 1 else range(4)
-                for q in quads:
-                    eng.dma_start(out=out_2[g, 4 * q : 4 * q + 4, :].bitcast(I32), in_=y_scales[g][32 * q : 32 * q + 4, :].bitcast(I32))
+                lo, hi = span(arg[2:])
+                words = out_1[g].rearrange("p m t -> p (m t)").bitcast(I32)
+                eng.dma_start(out=words[:, 128 * lo : 128 * hi], in_=y_codes[g][:, 128 * lo : 128 * hi].bitcast(I32))
+            elif kind == "q":
+                for q in [int(c) for c in arg]:
+                    eng.dma_start(out=out_2[:, 4 * q : 4 * q + 4, :].bitcast(I32), in_=y_scales[32 * q : 32 * q + 8, :].bitcast(I32))
             elif kind == "T":
                 s = int(arg)
                 words = x_raw[s // 4][:, s % 4, :].bitcast(F32)
@@ -199,101 +196,21 @@ def tile_sheared_right_basis_transform_g2_kernel(tc, images, even, odd, cos_tab,
             elif kind == "C":
                 grp = int(arg[0])
                 lo, hi = half(arg[1])
-                dst = y_grp[grp][:, lo:hi, :].rearrange("p (c i) t -> p c t i", i=2)
-                src = y[grp][:, :, lo:hi].rearrange("p t (c i) -> p c t i", i=2)
+                dst = y_grp[grp // 2][:, F * (grp % 2) + lo : F * (grp % 2) + hi, :].rearrange("p (c i) t -> p c t i", i=2)
+                src = (y[grp][:, :, lo:hi] if grp < 3 else last_y(slice(0, 4), lo, hi)).rearrange("p t (c i) -> p c t i", i=2)
                 if eng is nc.scalar:
                     eng.copy(out=dst, in_=src)
                 else:
                     eng.tensor_copy(out=dst, in_=src)
-            elif kind == "Y":
-                grp = int(arg[0])
-                g, b = divmod(grp, 2)
-                lo, hi = half(arg[1]) if len(arg) > 1 else (0, 512)
-                eng.quantize_mx(out=y_codes[grp][:, lo:hi].bitcast(FP8X4), scales=y_scales[g][:, F * b + lo : F * b + hi],
-                                in_=y_grp[grp][:, lo:hi, :].rearrange("p f t -> p (f t)"))
+            elif kind == "N":
+                g = int(arg[0])
+                lo, hi = span(arg[2:])
+                cols = slice(128 * lo, 128 * hi)
+                eng.quantize_mx(out=y_codes[g][:, cols].bitcast(FP8X4), scales=y_scales[4 * g :, cols],
+                                in_=y_grp[g][:, cols, :].rearrange("p f t -> p (f t)"))
 
-        queues = [(nc.sync, SP.split()), (nc.tensor, pe_steps), (nc.scalar, SC.split()), (nc.vector, VE.split()), (nc.gpsimd, GP.split())]
-        every = [step for eng, steps in queues for step in steps]
-
-        def covering(kind, s):
-            return [t for t in every if t[0] == kind and ":" not in t and "-" in t and span(t[1:])[0] <= s < span(t[1:])[1]]
-
-        def cols_meet(a, b):
-            la, ha = half(a) if a else (0, 512)
-            lb, hb = half(b) if b else (0, 512)
-            return la < hb and lb < ha
-
-        def cover_b(s, letter):
-            return [t for t in every if t[0] == "B" and cols_meet(t[1], letter) and span(t[2:])[0] <= s < span(t[2:])[1]]
-
-        def needs(step):
-            kind, arg = step[0], step[1:]
-            if kind == "Q":
-                return ["H" + arg if "H" + arg in every else "K" + arg, "win"] + [t for t in every if t[0] in "cs" and t[1] == str(int(arg[1:]) // 8)]
-            if kind == "B":
-                lo, hi = span(arg[1:])
-                return [t for t in every if t[0] == "Q" and cols_meet(t[1], arg[0]) and lo <= int(t[2:]) < hi] + [t for t in every if t[0] in "PR" and lo <= int(t[1:]) < hi]
-            if kind == "v":
-                lo, hi = span(arg[1:])
-                return [t for s in range(lo, hi) for t in cover_b(s, arg[0])]
-            if step == "win" or kind in "xwcs":
-                return []
-            if kind == "K":
-                return ["G" + arg] + [t for t in every if t[:2] == "Wo" and cols_meet(t[3:], arg[0])]
-            if kind in "TUVHG":
-                i = takers.index(step)
-                out = []
-                if i >= BANKS:
-                    old = takers[i - BANKS]
-                    out.append(reader[old[0]] + old[1:])
-                if kind in "HG":
-                    return out + covering("X", int(arg[1:])) + [t for t in every if t[0] == "W" and cols_meet(t[3:], arg[0]) and (kind == "H" or t[1] == "e")]
-                s = int(arg)
-                if kind == "T":
-                    return out + covering("x", s)
-                return out + covering("X", s) + [t for t in every if t[:2] == ("We" if kind == "U" else "Wo")]
-            if kind == "E":
-                s = int(arg)
-                return ["T" + arg] + (covering("X", s - 8) if s >= 8 else [])
-            if kind == "I":
-                return ["w" + arg[:2]]
-            if kind == "W":
-                return [t for t in every if t[0] == "I" and t[1:3] == arg[:2] and cols_meet(t[3:], arg[2:])]
-            if kind == "X":
-                lo, hi = span(arg)
-                return ["E%d" % s for s in range(lo, hi)]
-            if kind in "PR":
-                s = int(arg)
-                tab = "c" if kind == "P" else "s"
-                out = [("U" if kind == "P" else "V") + arg, "win"] + [t for t in every if t[0] == tab and t[1] == str(s // 8)]
-                return out
-            if kind == "A":
-                lo, hi = span(arg)
-                return ["P%d" % s for s in range(lo, hi)] + ["R%d" % s for s in range(lo, hi)]
-            if kind == "y":
-                lo, hi = span(arg)
-                return [t for s in range(lo, hi) for t in covering("A", s) + cover_b(s, "")]
-            if kind == "C":
-                grp = int(arg[0])
-                return [t for s in range(4 * grp, 4 * grp + 4) for t in covering("A", s) + cover_b(s, arg[1])]
-            if kind == "Y":
-                return [t for t in every if t[0] == "C" and t[1] == arg[0] and cols_meet(t[2:], arg[1:])]
-            if kind == "o":
-                return [t for t in every if t[0] == "Y" and t[1] == arg[0] and cols_meet(t[2:], arg[1:])]
-            if kind == "z":
-                return [t for t in every if t[0] == "Y" and int(t[1]) // 2 == int(arg[0])]
-
+        engines = {"SP": nc.sync, "PE": nc.tensor, "SC": nc.scalar, "VE": nc.vector, "GP": nc.gpsimd}
         make_identity(nc, ident[:])
         with tc.manual_schedule():
-            if True:
-                done = set()
-                at = [0] * len(queues)
-                while len(done) < len(every):
-                    moved = False
-                    for qi, (eng, steps) in enumerate(queues):
-                        while at[qi] < len(steps) and all(t in done for t in needs(steps[at[qi]])):
-                            emit(eng, steps[at[qi]])
-                            done.add(steps[at[qi]])
-                            at[qi] += 1
-                            moved = True
-                    assert moved
+            for item in ORDER.split():
+                emit(engines[item[:2]], item[3:])

@@ -17,7 +17,7 @@ FLOPS = 2 * 2 * B * H * W * F
 P = 128
 BANKS = 8
 
-ORDER = "SP:we0 SP:x0-2 SP:we1 SP:x2-4 SP:wo0 SP:wo1 SP:x4-6 SP:x6-8 SC:Ie0b VE:Ie0a SP:win PE:T0 SP:c0:0-2 VE:We0 PE:T1 SC:E0 VE:Ie1a SP:s0:0-2 SC:Ie1b VE:E1 PE:T2 SP:x8-10 VE:X0-2 PE:T3 SC:E2 VE:We1 SP:c0:2-4 VE:Io0a PE:U0 SC:E3 SP:s0:2-4 SC:Io1b VE:Io0b PE:U1 VE:Io1a SP:x10-12 PE:T4 VE:Wo0 PE:T5 SC:E4 VE:Wo1 SP:x12-14 PE:T6 SP:c1 SC:E5 PE:T7 VE:X2-4 SP:s1 SC:E6 VE:P0 PE:V0 SP:x14-16 PE:V1 SC:E7 VE:P1 PE:U2 VE:X4-6 PE:V2 VE:R0 PE:T8 VE:R1 PE:T9 VE:X6-8 SC:E8 PE:U3 VE:R2 GP:A0-2 SC:E9 PE:V3 VE:P2 PE:U4 VE:P3 PE:V4 VE:R3 PE:T10 VE:X8-10 SP:y0-2 PE:T11 SC:E10 VE:R4 GP:A2-4 PE:U5 SC:E11 VE:P4 PE:V5 VE:P5 PE:U6 VE:R5 PE:V6 VE:X10-12 PE:U7 SC:C0a SP:y2-4 VE:R6 GP:A4-6 PE:V7 PE:U8 VE:P6 SC:C0b PE:V8 VE:P7 PE:T12 VE:R7 PE:T13 VE:N0:0-2 SP:y4-6 SC:E12 VE:R8 GP:A6-8 PE:U9 SP:n0:0-2 SC:E13 VE:P8 PE:V9 VE:P9 PE:U10 VE:R9 PE:V10 VE:X12-14 PE:T14 SP:y6-8 PE:T15 VE:R10 GP:A8-10 SC:E14 PE:U11 VE:P10 SC:E15 PE:V11 SC:C1a VE:P11 PE:Ha12 VE:R11 PE:Ha13 SP:y8-10 VE:X14-16 SC:C1b VE:Qa12 GP:A10-12 PE:Ha14 VE:Qa13 PE:Ha15 VE:Qa14 PE:Hb12 VE:Qa15 PE:Hb13 GP:Ba12-14 VE:Qb12 PE:Hb14 SC:C2a SP:y10-12 PE:Hb15 VE:Qb13 GP:Ba14-16 VE:Qb14 SP:va12-14 SC:C2b VE:Qb15 VE:N0:2-6 SP:va14-16 SC:C3a VE:N0:6-8 VE:Bb12-14 SP:n0:2-8 VE:Bb14-16 SP:vb12-14 VE:N1:0-4 SC:C3e SP:vb14-16 VE:C3f SP:n1:0-4 VE:N1:4-6 VE:N1:6-8 SP:n1:4-6 SC:q23 SP:n1:6-8 SP:q01"
+ORDER = "SP:we0 SP:x0-2 SP:we1 SP:x2-4 SP:wo0 SP:wo1 SP:x4-6 SP:x6-8 SC:Ie0b VE:Ie0a SP:win PE:T0 SP:c0:0-2 VE:We0 PE:T1 SC:E0 VE:Ie1a SP:s0:0-2 SC:Ie1b VE:E1 PE:T2 SP:x8-10 VE:X0-2 PE:T3 SC:Io0b VE:We1 SP:c0:2-4 VE:Io0a PE:U0 SP:s0:2-4 SC:Io1b VE:Io1a PE:U1 VE:Wo0 SP:x10-12 PE:T4 SC:E2 VE:E3 PE:T5 SC:E4 VE:Wo1 SP:x12-14 PE:T6 SP:c1 SC:E5 VE:X2-4 PE:T7 SP:s1 SC:E6 VE:P0 PE:V0 SP:x14-16 PE:V1 SC:E7 VE:P1 PE:U2 VE:R0 SC:M8 PE:V2 VE:R1 SC:M9 PE:U3 VE:X4-6 PE:V3 VE:R2 GP:A0-2 PE:T8 SC:M10 VE:P2 PE:T9 PE:U4 SC:M11 VE:P3 PE:V4 SC:E8 VE:R3 SC:E9 PE:T10 VE:X6-8 SP:y0-2 PE:T11 SC:E10 VE:P4 GP:A2-4 PE:U5 SC:E11 VE:R4 PE:V5 VE:P5 PE:U6 PE:V6 VE:R5 PE:U7 VE:X8-12 SC:C0a SP:y2-4 PE:V7 PE:T12 VE:R6 GP:A4-6 SC:C0b PE:T13 VE:P6 PE:U8 VE:P7 SC:E12 PE:V8 VE:R7 SC:E13 PE:U9 VE:N0:0-4 SP:y4-6 PE:V9 VE:R8 GP:A6-8 SP:n0:0-4 PE:T14 VE:P8 PE:T15 VE:P9 SC:E14 PE:U10 VE:R9 SC:E15 PE:V10 VE:X12-14 SC:C1a SP:y6-8 PE:U11 VE:R10 GP:A8-10 PE:V11 VE:P10 PE:Ha12 SC:C1b VE:P11 PE:Ha13 VE:R11 VE:X14-16 SP:y8-10 VE:Qa12 GP:A10-12 PE:Ha14 VE:Qa13 PE:Ha15 VE:Qa14 PE:Hb12 VE:Qa15 PE:Hb13 GP:Ba12-14 VE:Qb12 PE:Hb14 SC:C2a SP:y10-12 PE:Hb15 VE:Qb13 GP:Ba14-16 VE:Qb14 SP:va12-14 SC:C2b VE:Qb15 VE:N0:4-8 SP:va14-16 SC:C3a VE:Bb12-14 SP:n0:4-8 VE:Bb14-16 SP:vb12-14 VE:N1:0-4 SC:C3e SP:vb14-16 VE:C3f SP:n1:0-4 VE:N1:4-6 VE:N1:6-8 SP:n1:4-6 SC:q012 SP:n1:6-8 SP:q3"
 
 
 def tile_sheared_right_basis_transform_g2_kernel(tc, images, even, odd, cos_tab, sin_tab, window, out_0, out_1, out_2):
@@ -137,14 +137,22 @@ def tile_sheared_right_basis_transform_g2_kernel(tc, images, even, odd, cos_tab,
             elif kind == "q":
                 for q in [int(c) for c in arg]:
                     eng.dma_start(out=out_2[:, 4 * q : 4 * q + 4, :].bitcast(I32), in_=y_scales[32 * q : 32 * q + 8, :].bitcast(I32))
+            elif kind == "M":
+                s = int(arg)
+                src = x_raw[s // 4][:, s % 4, :].bitcast(F32).rearrange("p (kg r u) -> p kg u r", kg=2, u=2)
+                dst = x_raw[s // 4 - 2][:, s % 4, :].bitcast(F32).rearrange("p (kg u r) -> p kg u r", kg=2, u=2)
+                eng.copy(out=dst, in_=src)
             elif kind == "T":
                 s = int(arg)
-                words = x_raw[s // 4][:, s % 4, :].bitcast(F32)
                 bank = banks[bank_of[step]]
                 for kg in range(2):
                     for u in range(2):
                         j = 2 * kg + u
-                        eng.transpose(bank[:, 128 * j : 128 * j + 128], words[:, 256 * kg + u : 256 * kg + 256 : 2], ident[:])
+                        if "SC:M" + arg in ORDER.split():
+                            src = x_raw[s // 4 - 2][:, s % 4, :].bitcast(F32)[:, 128 * j : 128 * j + 128]
+                        else:
+                            src = x_raw[s // 4][:, s % 4, :].bitcast(F32)[:, 256 * kg + u : 256 * kg + 256 : 2]
+                        eng.transpose(bank[:, 128 * j : 128 * j + 128], src, ident[:])
             elif kind in "UV":
                 s = int(arg)
                 bank = banks[bank_of[step]]

@@ -17,7 +17,7 @@ FLOPS = 2 * 2 * B * H * W * F
 P = 128
 BANKS = 8
 
-ORDER = "SP:we0 SP:x0-2 SP:we1 SP:x2-4 SP:wo0 SP:wo1 SP:x4-6 SP:x6-8 SC:Ie0b VE:Ie0a SP:win PE:T0 SP:c0:0-2 VE:We0 PE:T1 SC:E0 VE:Ie1a SP:s0:0-2 SC:Ie1b VE:E1 PE:T2 SP:x8-10 VE:X0-2 PE:T3 SC:Io0b VE:We1 SP:c0:2-4 VE:Io0a PE:U0 SP:s0:2-4 SC:Io1b VE:Io1a PE:U1 VE:Wo0 SP:x10-12 PE:T4 SC:E2 VE:E3 PE:T5 SC:E4 VE:Wo1 SP:x12-14 PE:T6 SP:c1 SC:E5 VE:X2-4 PE:T7 SP:s1 SC:E6 VE:P0 PE:V0 SP:x14-16 PE:V1 SC:E7 VE:P1 PE:U2 VE:R0 SC:M8 PE:V2 VE:R1 SC:M9 PE:U3 VE:X4-6 PE:V3 VE:R2 GP:A0-2 PE:T8 SC:M10 VE:P2 PE:T9 PE:U4 SC:M11 VE:P3 PE:V4 SC:E8 VE:R3 SC:E9 PE:T10 VE:X6-8 SP:y0-2 PE:T11 SC:E10 VE:P4 GP:A2-4 PE:U5 SC:E11 VE:R4 PE:V5 VE:P5 PE:U6 PE:V6 VE:R5 PE:U7 VE:X8-12 SC:C0a SP:y2-4 PE:V7 PE:T12 VE:R6 GP:A4-6 SC:C0b PE:T13 VE:P6 PE:U8 VE:P7 SC:E12 PE:V8 VE:R7 SC:E13 PE:U9 VE:N0:0-4 SP:y4-6 PE:V9 VE:R8 GP:A6-8 SP:n0:0-4 PE:T14 VE:P8 PE:T15 VE:P9 SC:E14 PE:U10 VE:R9 SC:E15 PE:V10 VE:X12-14 SC:C1a SP:y6-8 PE:U11 VE:R10 GP:A8-10 PE:V11 VE:P10 PE:Ha12 SC:C1b VE:P11 PE:Ha13 VE:R11 VE:X14-16 SP:y8-10 VE:Qa12 GP:A10-12 PE:Ha14 VE:Qa13 PE:Ha15 VE:Qa14 PE:Hb12 VE:Qa15 PE:Hb13 GP:Ba12-14 VE:Qb12 PE:Hb14 SC:C2a SP:y10-12 PE:Hb15 VE:Qb13 GP:Ba14-16 VE:Qb14 SP:va12-14 SC:C2b VE:Qb15 VE:N0:4-8 SP:va14-16 SC:C3a VE:Bb12-14 SP:n0:4-8 VE:Bb14-16 SP:vb12-14 VE:N1:0-4 SC:C3e SP:vb14-16 VE:C3f SP:n1:0-4 VE:N1:4-6 VE:N1:6-8 SP:n1:4-6 SC:q012 SP:n1:6-8 SP:q3"
+ORDER = "SC:win SP:we0 SP:x0-2 SP:we1 SP:x2-4 SP:wo0 SP:wo1 SP:x4-6 SC:Ie0b VE:Ie0a SP:x6-8 SP:c0:0-2 PE:T0 SP:s0:0-2 VE:We0 PE:T1 SC:E0 VE:Ie1a SP:x8-10 SC:Ie1b VE:E1 PE:T2 SP:c0:2-4 VE:X0-2 PE:T3 SC:Io0b VE:We1 SP:s0:2-4 VE:Io0a PE:U0 SP:x10-12 SC:Io1b VE:Io1a PE:U1 VE:Wo0 SP:x12-14 PE:T4 SC:E2 VE:E3 PE:T5 SP:c1 SC:E4 VE:Wo1 PE:T6 SP:s1 SC:E5 PE:T7 VE:X2-4 SP:x14-16 SC:E6 PE:V0 VE:P0 SC:E7 PE:V1 VE:P1 PE:U2 SC:M8 VE:R0 PE:V2 SC:M9 VE:R1 PE:U3 VE:X4-6 PE:V3 SC:M10 VE:R2 GP:A0-2 PE:T8 PE:T9 SC:M11 VE:P2 PE:U4 SC:E8 VE:P3 PE:V4 SC:E9 VE:R3 PE:T10 PE:T11 VE:X6-8 SP:y0-2 SC:E10 PE:U5 VE:P4 GP:A2-4 SC:E11 PE:V5 VE:R4 PE:U6 PE:V6 VE:P5 PE:U7 VE:R5 PE:V7 SC:C0a VE:X8-12 SP:y2-4 PE:T12 PE:T13 VE:R6 GP:A4-6 SC:C0b PE:U8 VE:P6 PE:V8 VE:R7 SC:E12 PE:T14 VE:P7 SC:E13 PE:T15 VE:N0:0-4 SC:E14 SP:y4-6 PE:U9 VE:R8 GP:A6-8 SC:E15 PE:V9 SP:n0:0-4 VE:P8 PE:U10 VE:P9 PE:V10 PE:U11 VE:R9 PE:V11 VE:X12-16 SC:C1a SP:y6-8 VE:R10 GP:A8-10 SC:C1b PE:Ha12 VE:P10 PE:Ha13 VE:R11 PE:Ha14 PE:Ha15 VE:P11 VE:N0:4-8 PE:Hb12 SP:y8-10 PE:Hb13 VE:Qa13 GP:A10-12 SP:n0:4-8 PE:Hb14 VE:Qa12 PE:Hb15 VE:Qa15 VE:Qa14 GP:Ba12-14 VE:Qb13 SC:C2a SP:y10-12 VE:Qb12 GP:Ba14-16 VE:Qb15 SP:va12-14 SC:C2b VE:Qb14 VE:Bb12-14 SC:C3a SP:va14-16 VE:Bb14-16 SP:vb12-14 VE:N1:0-4 SC:C3e SP:vb14-16 VE:C3f SP:n1:0-4 VE:N1:4-6 VE:N1:6-8 SP:n1:4-6 SC:q012 SP:n1:6-8 SP:q3"
 
 
 def tile_sheared_right_basis_transform_g2_kernel(tc, images, even, odd, cos_tab, sin_tab, window, out_0, out_1, out_2):

from contextlib import ExitStack

import concourse.mybir as mybir
from concourse.masks import make_identity

F32 = mybir.dt.float32
BF16 = mybir.dt.bfloat16
U32 = mybir.dt.uint32
I32 = mybir.dt.int32
U8 = mybir.dt.uint8
FP8X4 = mybir.dt.float8_e4m3fn_x4
MULT = mybir.AluOpType.mult
ADD = mybir.AluOpType.add

B, H, W, F = 2, 1024, 1024, 512
FLOPS = 2 * 2 * B * H * W * F
P = 128
BANKS = 8

ORDER = "SC:win SP:we0 SP:x0-2 SP:we1 SP:x2-4 SP:wo0 SP:wo1 SP:x4-6 SC:Ie0b VE:Ie0a SP:x6-8 SP:c0:0-2 PE:T0 SP:s0:0-2 VE:We0 PE:T1 SC:E0 VE:Ie1a SP:x8-10 SC:Ie1b VE:E1 PE:T2 SP:c0:2-4 VE:X0-2 PE:T3 SC:Io0b VE:We1 SP:s0:2-4 VE:Io0a PE:U0 SP:x10-12 SC:Io1b VE:Io1a PE:U1 VE:Wo0 SP:x12-14 PE:T4 SC:E2 VE:E3 PE:T5 SP:c1 SC:E4 VE:Wo1 PE:T6 SP:s1 SC:E5 PE:T7 VE:X2-4 SP:x14-16 SC:E6 PE:V0 VE:P0 SC:E7 PE:V1 VE:P1 PE:U2 SC:M8 VE:R0 PE:V2 SC:M9 VE:R1 PE:U3 VE:X4-6 PE:V3 SC:M10 VE:R2 GP:A0-2 PE:T8 PE:T9 SC:M11 VE:P2 PE:U4 SC:E8 VE:P3 PE:V4 SC:E9 VE:R3 PE:T10 PE:T11 VE:X6-8 SP:y0-2 SC:E10 PE:U5 VE:P4 GP:A2-4 SC:E11 PE:V5 VE:R4 PE:U6 PE:V6 VE:P5 PE:U7 VE:R5 PE:V7 SC:C0a VE:X8-12 SP:y2-4 PE:T12 PE:T13 VE:R6 GP:A4-6 SC:C0b PE:U8 VE:P6 PE:V8 VE:R7 SC:E12 PE:T14 VE:P7 SC:E13 PE:T15 VE:N0:0-4 SC:E14 SP:y4-6 PE:U9 VE:R8 GP:A6-8 SC:E15 PE:V9 SP:n0:0-4 VE:P8 PE:U10 VE:P9 PE:V10 PE:U11 VE:R9 PE:V11 VE:X12-16 SC:C1a SP:y6-8 VE:R10 GP:A8-10 SC:C1b PE:Ha12 VE:P10 PE:Ha13 VE:R11 PE:Ha14 PE:Ha15 VE:P11 VE:N0:4-8 PE:Hb12 SP:y8-10 PE:Hb13 VE:Qa13 GP:A10-12 SP:n0:4-8 PE:Hb14 VE:Qa12 PE:Hb15 VE:Qa15 VE:Qa14 GP:Ba12-14 VE:Qb13 SC:C2a SP:y10-12 VE:Qb12 GP:Ba14-16 VE:Qb15 SP:va12-14 SC:C2b VE:Qb14 VE:Bb12-14 SC:C3a SP:va14-16 VE:Bb14-16 SP:vb12-14 VE:N1:0-4 SC:C3e SP:vb14-16 VE:C3f SP:n1:0-4 VE:N1:4-6 VE:N1:6-8 SP:n1:4-6 SC:q012 SP:n1:6-8 SP:q3"


def tile_sheared_right_basis_transform_g2_kernel(tc, images, even, odd, cos_tab, sin_tab, window, out_0, out_1, out_2):
    nc = tc.nc
    with ExitStack() as ctx:
        sb = ctx.enter_context(tc.tile_pool(name="sb", bufs=1))
        ps = ctx.enter_context(tc.psum_pool(name="ps", bufs=1))

        def tiles(name, count, shape, dtype):
            return [sb.tile(shape, dtype, name="%s%d" % (name, i), align_bytes=64) for i in range(count)]

        ident = sb.tile([P, P], F32, name="ident")
        win = sb.tile([P, 2, 4], BF16, name="win")
        x_raw = tiles("x_raw", 4, [P, 4, W], BF16)
        x_grp = tiles("x_grp", 2, [P, 4, W], BF16)
        x_codes = tiles("x_codes", 4, [P, 4 * 256], U32)
        x_scales = tiles("x_scales", 4, [P, 4 * 256], U8)
        w_raw = tiles("w_raw", 4, [P, 4, F], BF16)
        w_grp = tiles("w_grp", 4, [P, F, 4], BF16)
        w_codes = tiles("w_codes", 4, [P, F], U32)
        w_scales = tiles("w_scales", 4, [P, F], U8)
        tabs = tiles("tabs", 2, [P, 2, 4, F], BF16)
        prod = tiles("prod", 3, [P, 2, 4, F], F32)
        last = tiles("last", 2, [P, 4, 2, F // 2], F32)

        def last_y(ts, c0, c1, side=0):
            return last[c0 // 256][:, ts, side, c0 % 256 : c0 % 256 + c1 - c0]

        cos_sb = [t[:, 0] for t in tabs]
        sin_sb = [t[:, 1] for t in tabs]
        y = [t[:, 0] for t in prod]
        vs = [t[:, 1] for t in prod]
        y_grp = tiles("y_grp", 2, [P, B * F, 4], BF16)
        y_codes = tiles("y_codes", 2, [P, B * F], U32)
        y_scales = sb.tile([P, B * F], U8, name="y_scales", align_bytes=64)
        banks = [ps.tile([P, 512], F32, name="bank%d" % i) for i in range(BANKS)]

        bank_of = {}
        pe_steps = [t[3:] for t in ORDER.split() if t[:2] == "PE"]
        takers = [t for t in pe_steps if t[0] != "K"]
        for i, step in enumerate(takers):
            bank_of[step] = i % BANKS
            if step[0] == "G":
                bank_of["K" + step[1:]] = i % BANKS
                bank_of["H" + step[1:]] = i % BANKS

        def span(text):
            lo, hi = text.split("-")
            return int(lo), int(hi)

        def half(letter):
            return {"a": (0, 256), "b": (256, 512), "c": (0, 128), "d": (128, 256), "e": (256, 384), "f": (384, 512)}[letter]

        def widx(text):
            return {"e": 0, "o": 2}[text[0]] + int(text[1])

        def rows(ap):
            return ap.rearrange("(p t) c -> p t c", t=4)

        def emit(eng, step):
            kind, arg = step[0], step[1:]
            if step == "win":
                eng.dma_start(out=win[:], in_=window.rearrange("(g p t) -> p g t", g=2, t=4))
            elif kind == "x":
                lo, hi = span(arg)
                grp = lo // 4
                g, b = divmod(grp, 2)
                eng.dma_start(out=x_raw[grp][:, lo % 4 : lo % 4 + hi - lo, :], in_=rows(images[b, 512 * g : 512 * g + 512, :])[:, lo % 4 : lo % 4 + hi - lo, :])
            elif kind == "w":
                kg = int(arg[1])
                src = even if arg[0] == "e" else odd
                eng.dma_start(out=w_raw[widx(arg)][:], in_=rows(src[512 * kg : 512 * kg + 512, :]))
            elif kind in "cs":
                g = int(arg[0])
                lo, hi = span(arg[2:]) if len(arg) > 1 else (0, 4)
                src, dst = (cos_tab, cos_sb) if kind == "c" else (sin_tab, sin_sb)
                eng.dma_start(out=dst[g][:, lo:hi, :], in_=rows(src[512 * g : 512 * g + 512, :])[:, lo:hi, :])
            elif kind == "y":
                lo, hi = span(arg)
                grp = lo // 4
                g, b = divmod(grp, 2)
                eng.dma_start(out=rows(out_0[b, 512 * g : 512 * g + 512, :])[:, lo % 4 : lo % 4 + hi - lo, :], in_=y[grp][:, lo % 4 : lo % 4 + hi - lo, :])
            elif kind == "v":
                c0, c1 = half(arg[0])
                lo, hi = span(arg[1:])
                grp = lo // 4
                g, b = divmod(grp, 2)
                eng.dma_start(out=rows(out_0[b, 512 * g : 512 * g + 512, :])[:, lo % 4 : lo % 4 + hi - lo, c0:c1], in_=last_y(slice(lo % 4, lo % 4 + hi - lo), c0, c1))
            elif kind in "HGK":
                c0, c1 = half(arg[0])
                s = int(arg[1:])
                bank = banks[bank_of[step]]
                for side in {"H": (0, 1), "G": (0,), "K": (1,)}[kind]:
                    for kg in range(2):
                        cols = slice(256 * (s % 4) + 128 * kg, 256 * (s % 4) + 128 * kg + 128)
                        wi = 2 * side + kg
                        eng.matmul_mx(out=bank[:, side * (c1 - c0) : (side + 1) * (c1 - c0)], lhsT=x_codes[s // 4][:, cols].bitcast(FP8X4), lhsT_scale=x_scales[s // 4][:, cols],
                                      rhs=w_codes[wi][:, c0:c1].bitcast(FP8X4), rhs_scale=w_scales[wi][:, c0:c1], start=(kg == 0), stop=(kg == 1))
            elif kind == "Q":
                c0, c1 = half(arg[0])
                s = int(arg[1:])
                g = s // 8
                bank = banks[bank_of["H" + arg]]
                eng.scalar_tensor_tensor(out=last[c0 // 256][:, s % 4, :, c0 % 256 : c0 % 256 + c1 - c0], in0=bank[:, : 2 * (c1 - c0)].rearrange("p (a f) -> p a f", a=2),
                                         scalar=win[:, g, s % 4 : s % 4 + 1], in1=tabs[g][:, :, s % 4, c0:c1], op0=MULT, op1=MULT)
            elif kind == "B":
                c0, c1 = half(arg[0])
                lo, hi = span(arg[1:])
                grp = lo // 4
                ts = slice(lo % 4, lo % 4 + hi - lo)
                eng.tensor_tensor(out=last_y(ts, c0, c1), in0=last_y(ts, c0, c1), in1=last_y(ts, c0, c1, 1), op=ADD)
            elif kind == "n":
                g = int(arg[0])
                lo, hi = span(arg[2:])
                words = out_1[g].rearrange("p m t -> p (m t)").bitcast(I32)
                eng.dma_start(out=words[:, 128 * lo : 128 * hi], in_=y_codes[g][:, 128 * lo : 128 * hi].bitcast(I32))
            elif kind == "q":
                for q in [int(c) for c in arg]:
                    eng.dma_start(out=out_2[:, 4 * q : 4 * q + 4, :].bitcast(I32), in_=y_scales[32 * q : 32 * q + 8, :].bitcast(I32))
            elif kind == "M":
                s = int(arg)
                src = x_raw[s // 4][:, s % 4, :].bitcast(F32).rearrange("p (kg r u) -> p kg u r", kg=2, u=2)
                dst = x_raw[s // 4 - 2][:, s % 4, :].bitcast(F32).rearrange("p (kg u r) -> p kg u r", kg=2, u=2)
                eng.copy(out=dst, in_=src)
            elif kind == "T":
                s = int(arg)
                bank = banks[bank_of[step]]
                for kg in range(2):
                    for u in range(2):
                        j = 2 * kg + u
                        if "SC:M" + arg in ORDER.split():
                            src = x_raw[s // 4 - 2][:, s % 4, :].bitcast(F32)[:, 128 * j : 128 * j + 128]
                        else:
                            src = x_raw[s // 4][:, s % 4, :].bitcast(F32)[:, 256 * kg + u : 256 * kg + 256 : 2]
                        eng.transpose(bank[:, 128 * j : 128 * j + 128], src, ident[:])
            elif kind in "UV":
                s = int(arg)
                bank = banks[bank_of[step]]
                for kg in range(2):
                    cols = slice(256 * (s % 4) + 128 * kg, 256 * (s % 4) + 128 * kg + 128)
                    wi = (0 if kind == "U" else 2) + kg
                    eng.matmul_mx(out=bank[:], lhsT=x_codes[s // 4][:, cols].bitcast(FP8X4), lhsT_scale=x_scales[s // 4][:, cols],
                                  rhs=w_codes[wi][:].bitcast(FP8X4), rhs_scale=w_scales[wi][:], start=(kg == 0), stop=(kg == 1))
            elif kind == "E":
                s = int(arg)
                bank = banks[bank_of["T" + arg]]
                dst = x_grp[(s // 4) % 2][:, s % 4, :].bitcast(F32).rearrange("p (kg r u) -> p kg r u", kg=2, u=2)
                src = bank[:].rearrange("p (kg u r) -> p kg r u", kg=2, u=2)
                if eng is nc.scalar:
                    eng.copy(out=dst, in_=src)
                else:
                    eng.tensor_copy(out=dst, in_=src)
            elif kind == "I":
                wi = widx(arg)
                lo, hi = half(arg[2])
                dst = w_grp[wi][:, lo:hi, :].rearrange("p (c i) t -> p c t i", i=4)
                src = w_raw[wi][:, :, lo:hi].rearrange("p t (c i) -> p c t i", i=4)
                if eng is nc.scalar:
                    eng.copy(out=dst, in_=src)
                else:
                    eng.tensor_copy(out=dst, in_=src)
            elif kind == "W":
                wi = widx(arg)
                lo, hi = half(arg[2]) if len(arg) > 2 else (0, 512)
                eng.quantize_mx(out=w_codes[wi][:, lo:hi].bitcast(FP8X4), scales=w_scales[wi][:, lo:hi], in_=w_grp[wi][:, lo:hi, :].rearrange("p f t -> p (f t)"))
            elif kind == "X":
                lo, hi = span(arg)
                grp = lo // 4
                cols = slice(256 * (lo % 4), 256 * (lo % 4 + hi - lo))
                eng.quantize_mx(out=x_codes[grp][:, cols].bitcast(FP8X4), scales=x_scales[grp][:, cols],
                                in_=x_grp[grp % 2][:, lo % 4 : lo % 4 + hi - lo, :].rearrange("p t w -> p (t w)"))
            elif kind in "PR":
                s = int(arg)
                g = s // 8
                bank = banks[bank_of[("U" if kind == "P" else "V") + arg]]
                dst = y[s // 4] if kind == "P" else vs[s // 4]
                tab = cos_sb if kind == "P" else sin_sb
                eng.scalar_tensor_tensor(out=dst[:, s % 4, :], in0=bank[:], scalar=win[:, g, s % 4 : s % 4 + 1], in1=tab[g][:, s % 4, :], op0=MULT, op1=MULT)
            elif kind == "A":
                lo, hi = span(arg)
                grp = lo // 4
                ts = slice(lo % 4, lo % 4 + hi - lo)
                eng.tensor_tensor(out=y[grp][:, ts, :], in0=y[grp][:, ts, :], in1=vs[grp][:, ts, :], op=ADD)
            elif kind == "C":
                grp = int(arg[0])
                lo, hi = half(arg[1])
                dst = y_grp[grp // 2][:, F * (grp % 2) + lo : F * (grp % 2) + hi, :].rearrange("p (c i) t -> p c t i", i=2)
                src = (y[grp][:, :, lo:hi] if grp < 3 else last_y(slice(0, 4), lo, hi)).rearrange("p t (c i) -> p c t i", i=2)
                if eng is nc.scalar:
                    eng.copy(out=dst, in_=src)
                else:
                    eng.tensor_copy(out=dst, in_=src)
            elif kind == "N":
                g = int(arg[0])
                lo, hi = span(arg[2:])
                cols = slice(128 * lo, 128 * hi)
                eng.quantize_mx(out=y_codes[g][:, cols].bitcast(FP8X4), scales=y_scales[4 * g :, cols],
                                in_=y_grp[g][:, cols, :].rearrange("p f t -> p (f t)"))

        engines = {"SP": nc.sync, "PE": nc.tensor, "SC": nc.scalar, "VE": nc.vector, "GP": nc.gpsimd}
        make_identity(nc, ident[:])
        with tc.manual_schedule():
            for item in ORDER.split():
                emit(engines[item[:2]], item[3:])
